import numpy as np
import ml_dtypes


def mxq(x, axis, fmt="e4m3"):
    dtype, down = {"e4m3": (ml_dtypes.float8_e4m3fn, 7), "e5m2": (ml_dtypes.float8_e5m2, 14)}[fmt]
    v = np.moveaxis(np.asarray(x, np.float32).astype(ml_dtypes.bfloat16).astype(np.float64), axis, -1)
    blocks = v.reshape(v.shape[:-1] + (-1, 32))
    amax = np.abs(blocks).max(-1, keepdims=True)
    byte = np.maximum(np.where(amax > 0, np.frexp(amax)[1] - 1 + 127, 0) - down, 1)
    scale = np.exp2(byte - 127.0)
    codes = (blocks / scale).astype(np.float32).astype(dtype).astype(np.float64)
    return np.moveaxis((codes * scale).reshape(v.shape), -1, axis)


WIDE = False


def mx_kscale(k, group=512):
    if not WIDE:
        return np.ones(k)
    levels = np.array([18, -18])
    if group != 512:
        return np.exp2(np.random.permutation(np.resize(levels, k // group))).repeat(group)
    if k % 512:
        return np.exp2(np.random.permutation(np.resize(levels, k // 32))).repeat(32)
    a = np.empty((k // 512, 16))
    for p in range(k // 512):
        a[p, :8] = np.random.permutation(np.resize(levels, 8))
        for g in range(8):
            far = levels[np.abs(levels - a[p, g]) >= 10]
            a[p, g + 8] = far[np.random.randint(len(far))]
    return np.exp2(a.ravel()).repeat(32)


def f64(x):
    return np.asarray(x).astype(np.float64)


def sigmoid(v):
    return 1.0 / (1.0 + np.exp(-v))


G, D, M, N = 4, 128, 128, 512


def setup_inputs():
    n = np.random.standard_normal
    s_d = mx_kscale(D, 0)
    return {
        "h": (n((G, D, N)) * s_d[:, None]).astype(np.float32),
        "wr": (n((G, D, M)) / np.sqrt(D) / s_d[:, None]).astype(np.float32),
        "wi": (n((G, D, M)) / np.sqrt(D) / s_d[:, None]).astype(np.float32),
        "xh": (n((G, M, N))).astype(np.float32),
        "hp": (n((G, M, N))).astype(np.float32),
        "la": (-np.random.uniform(0.3, 3.0, (G, M, 1))).astype(np.float32),
        "br": (0.5 * n((G, M, 1))).astype(np.float32),
        "bi": (0.5 * n((G, M, 1))).astype(np.float32),
    }


def reference(h, wr, wi, xh, hp, la, br, bi):
    wrq = mxq(f64(wr), 1, "e4m3")
    hq = mxq(f64(h), 1, "e4m3")
    zr = wrq.transpose(0, 2, 1) @ hq
    wiq = mxq(f64(wi), 1, "e4m3")
    zi = wiq.transpose(0, 2, 1) @ hq
    a = np.exp(f64(la) * sigmoid(zr + f64(br)))
    y = a * f64(hp) + np.sqrt(1.0 - a * a) * sigmoid(zi + f64(bi)) * f64(xh)
    return y

@@ -1,0 +1,159 @@
+from contextlib import ExitStack
+
+import concourse.mybir as mybir
+
+G, D, M, N = 4, 128, 128, 512
+FLOPS = 2 * 2 * G * D * M * N
+
+F32 = mybir.dt.float32
+BF16 = mybir.dt.bfloat16
+U32 = mybir.dt.uint32
+U8 = mybir.dt.uint8
+FP8X4 = mybir.dt.float8_e4m3fn_x4
+ACT = mybir.ActivationFunctionType
+ALU = mybir.AluOpType
+
+P = 128
+PACK = 4
+ROWS = D // PACK
+N_MM = 128
+CHUNKS = ((0, 256), (256, 512))
+PIECE = 256
+VECTOR_SQUARES = 3
+
+
+def tile_rows_cell_rglru_kernel(tc, h, wr, wi, xh, hp, la, br, bi, out):
+    nc = tc.nc
+
+    with ExitStack() as ctx:
+        sb = ctx.enter_context(tc.tile_pool(name="sb", bufs=1))
+        ps = ctx.enter_context(tc.psum_pool(name="ps", bufs=1))
+        ctx.enter_context(tc.manual_schedule())
+
+        def load_operand(name, src):
+            width = src.shape[2]
+            raw = sb.tile([P, PACK, width], F32, name=name + "_raw")
+            nc.sync.dma_start(out=raw[:], in_=src.rearrange("g (p j) w -> (g p) j w", j=PACK))
+            return raw
+
+        def interleave(name, raw):
+            width = raw.shape[2]
+            grouped = sb.tile([P, width * PACK], BF16, name=name + "_bf", align_bytes=64)
+            nc.vector.tensor_copy(
+                out=grouped[:].rearrange("p (c i j) -> p c j i", i=4, j=PACK),
+                in_=raw[:].rearrange("p j (c i) -> p c j i", i=4),
+            )
+            return grouped
+
+        def quantise(name, grouped):
+            width = grouped.shape[1] // PACK
+            codes = sb.tile([P, width], U32, name=name + "_codes", align_bytes=64)
+            scales = sb.tile([P, width], U8, name=name + "_scales", align_bytes=64)
+            nc.vector.quantize_mx(out=codes[:].bitcast(FP8X4), scales=scales[:], in_=grouped[:])
+            return codes, scales
+
+        def gate_product(bank, g, w_mx, h_mx, n0, n1):
+            rows = slice(ROWS * g, ROWS * (g + 1))
+            for c in range(0, n1 - n0, N_MM):
+                nc.tensor.matmul_mx(
+                    out=bank[:, n0 + c : n0 + c + N_MM],
+                    lhsT=w_mx[0][rows, :].bitcast(FP8X4),
+                    lhsT_scale=w_mx[1][rows, :],
+                    rhs=h_mx[0][rows, c : c + N_MM].bitcast(FP8X4),
+                    rhs_scale=h_mx[1][rows, c : c + N_MM],
+                    start=True,
+                    stop=True,
+                )
+
+        z_r = [ps.tile([P, N], F32, name="zr%d" % g) for g in range(G)]
+        z_i = [ps.tile([P, N], F32, name="zi%d" % g) for g in range(G)]
+        t_r = sb.tile([P, G, N], F32, name="t_r")
+        t_i = sb.tile([P, G, N], F32, name="t_i")
+        a = sb.tile([P, G, N], F32, name="a")
+        a_cap = sb.tile([P, G, N], F32, name="a_cap")
+        a_sq = sb.tile([P, G, N], F32, name="a_sq")
+        root = sb.tile([P, G, N], F32, name="root")
+        kept = sb.tile([P, G, N], F32, name="kept")
+        gated = sb.tile([P, G, N], F32, name="gated")
+        fresh = sb.tile([P, G, N], F32, name="fresh")
+        y = sb.tile([P, G, N], F32, name="y")
+        hp_sb = sb.tile([P, G, N], F32, name="hp_sb")
+        xh_sb = sb.tile([P, G, N], F32, name="xh_sb")
+        rows_in = sb.tile([P, P], F32, name="rows_in", align_bytes=64)
+        cols = sb.tile([P, P], F32, name="cols", align_bytes=64)
+        half = sb.tile([P, P], F32, name="half", align_bytes=64)
+        warm_in = sb.tile([P, 8], F32, name="warm_in")
+        warm_out = sb.tile([P, 8], F32, name="warm_out")
+
+        nc.gpsimd.memset(rows_in[:], 0.0)
+        nc.gpsimd.memset(warm_in[:], 0.0)
+        nc.scalar.activation(warm_out[:, 0:1], warm_in[:, 0:1], ACT.Tanh)
+
+        wr_raw = load_operand("wr", wr)
+        for r, vec in enumerate((br, la, bi)):
+            nc.sync.dma_start(
+                out=rows_in[r:P:32, :].rearrange("q (g j) -> q g j", g=G),
+                in_=vec.rearrange("g (q j) o -> q g (j o)", q=4),
+            )
+        h_raw = [load_operand("h%d" % n0, h[:, :, n0:n1]) for n0, n1 in CHUNKS]
+        wi_raw = load_operand("wi", wi)
+        for n0, n1 in CHUNKS:
+            nc.sync.dma_start(out=hp_sb[:, :, n0:n1], in_=hp[:, :, n0:n1].rearrange("g m n -> m g n"))
+        for g0 in (0, 2):
+            nc.sync.dma_start(out=xh_sb[:, g0 : g0 + 2, :], in_=xh[g0 : g0 + 2].rearrange("g m n -> m g n"))
+
+        wr_bf = interleave("wr", wr_raw)
+        nc.vector.transpose(cols[:], rows_in[:])
+        wr_mx = quantise("wr", wr_bf)
+        nc.vector.tensor_scalar(half[:], cols[:], 0.5, None, ALU.mult)
+
+        def param(r, g):
+            return half[:, 32 * g + r : 32 * g + r + 1]
+
+        h_mx = []
+        for k, (n0, n1) in enumerate(CHUNKS):
+            h_mx.append(quantise("h%d" % n0, interleave("h%d" % n0, h_raw[k])))
+            for g in range(G):
+                gate_product(z_r[g], g, wr_mx, h_mx[k], n0, n1)
+            for g in range(G):
+                nc.scalar.activation(t_r[:, g, n0:n1], z_r[g][:, n0:n1], ACT.Tanh, bias=param(0, g), scale=0.5)
+            for g in range(G):
+                nc.scalar.activation(a[:, g, n0:n1], t_r[:, g, n0:n1], ACT.Exp, bias=param(1, g), scale=param(1, g))
+
+        wi_mx = quantise("wi", interleave("wi", wi_raw))
+        for g in range(G):
+            for k, (n0, n1) in enumerate(CHUNKS):
+                gate_product(z_i[g], g, wi_mx, h_mx[k], n0, n1)
+        for g in range(G):
+            nc.scalar.activation(t_i[:, g, :], z_i[g][:], ACT.Tanh, bias=param(2, g), scale=0.5)
+
+        for n0, n1 in CHUNKS:
+            for g0 in (0, 2):
+                part = (slice(None), slice(g0, g0 + 2), slice(n0, n1))
+                nc.vector.tensor_scalar(a_cap[part], a[part], 1.0, None, ALU.min)
+                nc.vector.tensor_tensor(kept[part], a[part], hp_sb[part], ALU.mult)
+
+        pieces = [(slice(None), g, slice(n0, n0 + PIECE)) for g in range(G) for n0 in range(0, N, PIECE)]
+        for part in pieces[:VECTOR_SQUARES]:
+            nc.vector.tensor_tensor(a_sq[part], a_cap[part], a_cap[part], ALU.mult)
+        for g in range(G):
+            nc.vector.scalar_tensor_tensor(gated[:, g, :], t_i[:, g, :], 1.0, xh_sb[:, g, :], ALU.add, ALU.mult)
+
+        def finish(k):
+            part = pieces[k]
+            nc.vector.tensor_tensor(y[part], fresh[part], kept[part], ALU.add)
+            g = part[1]
+            if g == G - 1:
+                nc.sync.dma_start(out=out[g, :, part[2]], in_=y[part])
+            elif part[2].stop == N:
+                nc.sync.dma_start(out=out[g], in_=y[:, g, :])
+
+        for k, part in enumerate(pieces):
+            nc.scalar.activation(root[part], a_sq[part], ACT.Sqrt, bias=1.0, scale=-1.0)
+            ahead = k + 2
+            if VECTOR_SQUARES <= ahead < len(pieces):
+                nc.scalar.activation(a_sq[pieces[ahead]], a_cap[pieces[ahead]], ACT.Square)
+            nc.vector.scalar_tensor_tensor(fresh[part], root[part], 0.5, gated[part], ALU.mult, ALU.mult)
+            if k > 0:
+                finish(k - 1)
+        finish(len(pieces) - 1)

@@ -17,9 +17,12 @@ P = 128
 PACK = 4
 ROWS = D // PACK
 N_MM = 128
-CHUNKS = ((0, 256), (256, 512))
-PIECE = 256
-VECTOR_SQUARES = 3
+CHUNKS = ((0, 128), (128, 256), (256, 512))
+WIDTHS = (128, 128, 256, 512, 512, 256, 128, 128)
+VECTOR_SQUARED = 1024
+SCALAR_TAIL = (("s", 0), ("s", 1), ("s", 2), ("s", 3), ("q", 1024, 1536), ("q", 1536, 1792), ("s", 4), ("q", 1792, 2048), ("s", 5), ("s", 6), ("s", 7))
+VECTOR_TAIL = (("m", 0), ("m", 1), ("y", 0), ("m", 2), ("y", 1), ("m", 3), ("y", 2), ("y", 3), ("m", 4), ("m", 5), ("y", 4), ("m", 6), ("y", 5), ("m", 7), ("y", 6), ("y", 7))
+STORES = ((0, 512), (512, 1024), (1024, 1536), (1536, 1792), (1792, 1920), (1920, 2048))
 
 
 def tile_rows_cell_rglru_kernel(tc, h, wr, wi, xh, hp, la, br, bi, out):
@@ -52,9 +55,9 @@ def tile_rows_cell_rglru_kernel(tc, h, wr, wi, xh, hp, la, br, bi, out):
             nc.vector.quantize_mx(out=codes[:].bitcast(FP8X4), scales=scales[:], in_=grouped[:])
             return codes, scales
 
-        def gate_product(bank, g, w_mx, h_mx, n0, n1):
+        def gate_product(bank, g, w_mx, h_mx, n0, c):
             rows = slice(ROWS * g, ROWS * (g + 1))
-            for c in range(0, n1 - n0, N_MM):
+            if True:
                 nc.tensor.matmul_mx(
                     out=bank[:, n0 + c : n0 + c + N_MM],
                     lhsT=w_mx[0][rows, :].bitcast(FP8X4),
@@ -90,70 +93,106 @@ def tile_rows_cell_rglru_kernel(tc, h, wr, wi, xh, hp, la, br, bi, out):
         nc.scalar.activation(warm_out[:, 0:1], warm_in[:, 0:1], ACT.Tanh)
 
         wr_raw = load_operand("wr", wr)
+        h_raw = [load_operand("h0", h[:, :, 0 : CHUNKS[0][1]])]
         for r, vec in enumerate((br, la, bi)):
             nc.sync.dma_start(
                 out=rows_in[r:P:32, :].rearrange("q (g j) -> q g j", g=G),
                 in_=vec.rearrange("g (q j) o -> q g (j o)", q=4),
             )
-        h_raw = [load_operand("h%d" % n0, h[:, :, n0:n1]) for n0, n1 in CHUNKS]
+        h_raw.append(load_operand("h1", h[:, :, CHUNKS[1][0] : CHUNKS[1][1]]))
         wi_raw = load_operand("wi", wi)
-        for n0, n1 in CHUNKS:
-            nc.sync.dma_start(out=hp_sb[:, :, n0:n1], in_=hp[:, :, n0:n1].rearrange("g m n -> m g n"))
+        h_raw.append(load_operand("h2", h[:, :, CHUNKS[2][0] : CHUNKS[2][1]]))
+        for g0 in (0, 2):
+            nc.sync.dma_start(out=hp_sb[:, g0 : g0 + 2, :], in_=hp[g0 : g0 + 2].rearrange("g m n -> m g n"))
         for g0 in (0, 2):
             nc.sync.dma_start(out=xh_sb[:, g0 : g0 + 2, :], in_=xh[g0 : g0 + 2].rearrange("g m n -> m g n"))
 
-        wr_bf = interleave("wr", wr_raw)
-        nc.vector.transpose(cols[:], rows_in[:])
-        wr_mx = quantise("wr", wr_bf)
-        nc.vector.tensor_scalar(half[:], cols[:], 0.5, None, ALU.mult)
+        wr_mx = quantise("wr", interleave("wr", wr_raw))
 
         def param(r, g):
             return half[:, 32 * g + r : 32 * g + r + 1]
 
-        h_mx = []
-        for k, (n0, n1) in enumerate(CHUNKS):
-            h_mx.append(quantise("h%d" % n0, interleave("h%d" % n0, h_raw[k])))
-            for g in range(G):
-                gate_product(z_r[g], g, wr_mx, h_mx[k], n0, n1)
+        def products(banks, w_mx, k):
+            n0, n1 = CHUNKS[k]
+            for g0 in (0, 2):
+                for c in range(0, n1 - n0, N_MM):
+                    for g in (g0, g0 + 1):
+                        gate_product(banks[g], g, w_mx, h_mx[k], n0, c)
+
+        def decay(k):
+            n0, n1 = CHUNKS[k]
             for g in range(G):
                 nc.scalar.activation(t_r[:, g, n0:n1], z_r[g][:, n0:n1], ACT.Tanh, bias=param(0, g), scale=0.5)
             for g in range(G):
                 nc.scalar.activation(a[:, g, n0:n1], t_r[:, g, n0:n1], ACT.Exp, bias=param(1, g), scale=param(1, g))
 
+        def input_gate(n0, n1):
+            for g in range(G):
+                nc.scalar.activation(t_i[:, g, n0:n1], z_i[g][:, n0:n1], ACT.Tanh, bias=param(2, g), scale=0.5)
+
+        split = CHUNKS[-1][0]
+        h_bf = interleave("h0", h_raw[0])
+        nc.vector.transpose(cols[:], rows_in[:])
+        nc.scalar.activation(half[:], cols[:], ACT.Copy, scale=0.5)
+        h_mx = [quantise("h0", h_bf)]
+        products(z_r, wr_mx, 0)
+        decay(0)
+        h_mx.append(quantise("h1", interleave("h1", h_raw[1])))
+        products(z_r, wr_mx, 1)
+        decay(1)
         wi_mx = quantise("wi", interleave("wi", wi_raw))
-        for g in range(G):
-            for k, (n0, n1) in enumerate(CHUNKS):
-                gate_product(z_i[g], g, wi_mx, h_mx[k], n0, n1)
-        for g in range(G):
-            nc.scalar.activation(t_i[:, g, :], z_i[g][:], ACT.Tanh, bias=param(2, g), scale=0.5)
+        products(z_i, wi_mx, 0)
+        products(z_i, wi_mx, 1)
+        input_gate(0, split)
+        h_mx.append(quantise("h2", interleave("h2", h_raw[2])))
+        products(z_r, wr_mx, 2)
+        products(z_i, wi_mx, 2)
+        decay(2)
+        input_gate(split, N)
 
-        for n0, n1 in CHUNKS:
-            for g0 in (0, 2):
-                part = (slice(None), slice(g0, g0 + 2), slice(n0, n1))
-                nc.vector.tensor_scalar(a_cap[part], a[part], 1.0, None, ALU.min)
-                nc.vector.tensor_tensor(kept[part], a[part], hp_sb[part], ALU.mult)
+        def cap(g0, g1, n0, n1):
+            nc.vector.tensor_scalar(a_cap[:, g0:g1, n0:n1], a[:, g0:g1, n0:n1], 1.0, None, ALU.min)
 
-        pieces = [(slice(None), g, slice(n0, n0 + PIECE)) for g in range(G) for n0 in range(0, N, PIECE)]
-        for part in pieces[:VECTOR_SQUARES]:
-            nc.vector.tensor_tensor(a_sq[part], a_cap[part], a_cap[part], ALU.mult)
-        for g in range(G):
-            nc.vector.scalar_tensor_tensor(gated[:, g, :], t_i[:, g, :], 1.0, xh_sb[:, g, :], ALU.add, ALU.mult)
+        def keep(g0, g1, n0, n1):
+            nc.vector.tensor_tensor(kept[:, g0:g1, n0:n1], a[:, g0:g1, n0:n1], hp_sb[:, g0:g1, n0:n1], ALU.mult)
 
-        def finish(k):
-            part = pieces[k]
-            nc.vector.tensor_tensor(y[part], fresh[part], kept[part], ALU.add)
-            g = part[1]
-            if g == G - 1:
-                nc.sync.dma_start(out=out[g, :, part[2]], in_=y[part])
-            elif part[2].stop == N:
-                nc.sync.dma_start(out=out[g], in_=y[:, g, :])
+        def flat(t, c0, c1):
+            return t[:].rearrange("p g n -> p (g n)")[:, c0:c1]
 
-        for k, part in enumerate(pieces):
-            nc.scalar.activation(root[part], a_sq[part], ACT.Sqrt, bias=1.0, scale=-1.0)
-            ahead = k + 2
-            if VECTOR_SQUARES <= ahead < len(pieces):
-                nc.scalar.activation(a_sq[pieces[ahead]], a_cap[pieces[ahead]], ACT.Square)
-            nc.vector.scalar_tensor_tensor(fresh[part], root[part], 0.5, gated[part], ALU.mult, ALU.mult)
-            if k > 0:
-                finish(k - 1)
-        finish(len(pieces) - 1)
+        def square(g0, g1, n0, n1):
+            nc.vector.tensor_tensor(a_sq[:, g0:g1, n0:n1], a_cap[:, g0:g1, n0:n1], a_cap[:, g0:g1, n0:n1], ALU.mult)
+
+        def gate(g0, g1, n0, n1):
+            part = (slice(None), slice(g0, g1), slice(n0, n1))
+            nc.vector.scalar_tensor_tensor(gated[part], t_i[part], 1.0, xh_sb[part], ALU.add, ALU.mult)
+
+        cap(0, 4, 0, split)
+        keep(0, 2, 0, split)
+        square(0, 2, 0, split)
+        keep(2, 4, 0, split)
+        gate(0, 2, 0, split)
+        cap(0, 2, split, N)
+        keep(0, 2, split, N)
+        square(0, 2, split, N)
+        gate(2, 4, 0, split)
+        cap(2, 4, split, N)
+        keep(2, 4, split, N)
+        gate(0, 4, split, N)
+
+        edges = [sum(WIDTHS[:k]) for k in range(len(WIDTHS) + 1)]
+        for step in SCALAR_TAIL:
+            if step[0] == "q":
+                nc.scalar.activation(flat(a_sq, step[1], step[2]), flat(a_cap, step[1], step[2]), ACT.Square)
+            else:
+                c0, c1 = edges[step[1]], edges[step[1] + 1]
+                nc.scalar.activation(flat(root, c0, c1), flat(a_sq, c0, c1), ACT.Sqrt, bias=1.0, scale=-1.0)
+        for kind, k in VECTOR_TAIL:
+            c0, c1 = edges[k], edges[k + 1]
+            if kind == "m":
+                nc.vector.scalar_tensor_tensor(flat(fresh, c0, c1), flat(root, c0, c1), 0.5, flat(gated, c0, c1), ALU.mult, ALU.mult)
+            else:
+                nc.vector.tensor_tensor(flat(y, c0, c1), flat(fresh, c0, c1), flat(kept, c0, c1), ALU.add)
+                for s0, s1 in STORES:
+                    if c0 < s1 <= c1:
+                        g = s0 // N
+                        (nc.scalar if s1 == G * N else nc.sync).dma_start(out=out[g, :, s0 - g * N : s1 - g * N], in_=flat(y, s0, s1))

@@ -114,10 +114,9 @@ def tile_rows_cell_rglru_kernel(tc, h, wr, wi, xh, hp, la, br, bi, out):
 
         def products(banks, w_mx, k):
             n0, n1 = CHUNKS[k]
-            for g0 in (0, 2):
-                for c in range(0, n1 - n0, N_MM):
-                    for g in (g0, g0 + 1):
-                        gate_product(banks[g], g, w_mx, h_mx[k], n0, c)
+            for c in range(0, n1 - n0, N_MM):
+                for g in range(G):
+                    gate_product(banks[g], g, w_mx, h_mx[k], n0, c)
 
         def decay(k):
             n0, n1 = CHUNKS[k]
@@ -131,10 +130,9 @@ def tile_rows_cell_rglru_kernel(tc, h, wr, wi, xh, hp, la, br, bi, out):
                 nc.scalar.activation(t_i[:, g, n0:n1], z_i[g][:, n0:n1], ACT.Tanh, bias=param(2, g), scale=0.5)
 
         split = CHUNKS[-1][0]
-        h_bf = interleave("h0", h_raw[0])
-        nc.vector.transpose(cols[:], rows_in[:])
-        nc.scalar.activation(half[:], cols[:], ACT.Copy, scale=0.5)
-        h_mx = [quantise("h0", h_bf)]
+        h_mx = [quantise("h0", interleave("h0", h_raw[0]))]
+        nc.scalar.activation(cols[:], rows_in[:], ACT.Copy, scale=0.5)
+        nc.vector.transpose(half[:], cols[:])
         products(z_r, wr_mx, 0)
         decay(0)
         h_mx.append(quantise("h1", interleave("h1", h_raw[1])))

from contextlib import ExitStack

import concourse.mybir as mybir

G, D, M, N = 4, 128, 128, 512
FLOPS = 2 * 2 * G * D * M * N

F32 = mybir.dt.float32
BF16 = mybir.dt.bfloat16
U32 = mybir.dt.uint32
U8 = mybir.dt.uint8
FP8X4 = mybir.dt.float8_e4m3fn_x4
ACT = mybir.ActivationFunctionType
ALU = mybir.AluOpType

P = 128
PACK = 4
ROWS = D // PACK
N_MM = 128
CHUNKS = ((0, 128), (128, 256), (256, 512))
WIDTHS = (128, 128, 256, 512, 512, 256, 128, 128)
VECTOR_SQUARED = 1024
SCALAR_TAIL = (("s", 0), ("s", 1), ("s", 2), ("s", 3), ("q", 1024, 1536), ("q", 1536, 1792), ("s", 4), ("q", 1792, 2048), ("s", 5), ("s", 6), ("s", 7))
VECTOR_TAIL = (("m", 0), ("m", 1), ("y", 0), ("m", 2), ("y", 1), ("m", 3), ("y", 2), ("y", 3), ("m", 4), ("m", 5), ("y", 4), ("m", 6), ("y", 5), ("m", 7), ("y", 6), ("y", 7))
STORES = ((0, 512), (512, 1024), (1024, 1536), (1536, 1792), (1792, 1920), (1920, 2048))


def tile_rows_cell_rglru_kernel(tc, h, wr, wi, xh, hp, la, br, bi, out):
    nc = tc.nc

    with ExitStack() as ctx:
        sb = ctx.enter_context(tc.tile_pool(name="sb", bufs=1))
        ps = ctx.enter_context(tc.psum_pool(name="ps", bufs=1))
        ctx.enter_context(tc.manual_schedule())

        def load_operand(name, src):
            width = src.shape[2]
            raw = sb.tile([P, PACK, width], F32, name=name + "_raw")
            nc.sync.dma_start(out=raw[:], in_=src.rearrange("g (p j) w -> (g p) j w", j=PACK))
            return raw

        def interleave(name, raw):
            width = raw.shape[2]
            grouped = sb.tile([P, width * PACK], BF16, name=name + "_bf", align_bytes=64)
            nc.vector.tensor_copy(
                out=grouped[:].rearrange("p (c i j) -> p c j i", i=4, j=PACK),
                in_=raw[:].rearrange("p j (c i) -> p c j i", i=4),
            )
            return grouped

        def quantise(name, grouped):
            width = grouped.shape[1] // PACK
            codes = sb.tile([P, width], U32, name=name + "_codes", align_bytes=64)
            scales = sb.tile([P, width], U8, name=name + "_scales", align_bytes=64)
            nc.vector.quantize_mx(out=codes[:].bitcast(FP8X4), scales=scales[:], in_=grouped[:])
            return codes, scales

        def gate_product(bank, g, w_mx, h_mx, n0, c):
            rows = slice(ROWS * g, ROWS * (g + 1))
            if True:
                nc.tensor.matmul_mx(
                    out=bank[:, n0 + c : n0 + c + N_MM],
                    lhsT=w_mx[0][rows, :].bitcast(FP8X4),
                    lhsT_scale=w_mx[1][rows, :],
                    rhs=h_mx[0][rows, c : c + N_MM].bitcast(FP8X4),
                    rhs_scale=h_mx[1][rows, c : c + N_MM],
                    start=True,
                    stop=True,
                )

        z_r = [ps.tile([P, N], F32, name="zr%d" % g) for g in range(G)]
        z_i = [ps.tile([P, N], F32, name="zi%d" % g) for g in range(G)]
        t_r = sb.tile([P, G, N], F32, name="t_r")
        t_i = sb.tile([P, G, N], F32, name="t_i")
        a = sb.tile([P, G, N], F32, name="a")
        a_cap = sb.tile([P, G, N], F32, name="a_cap")
        a_sq = sb.tile([P, G, N], F32, name="a_sq")
        root = sb.tile([P, G, N], F32, name="root")
        kept = sb.tile([P, G, N], F32, name="kept")
        gated = sb.tile([P, G, N], F32, name="gated")
        fresh = sb.tile([P, G, N], F32, name="fresh")
        y = sb.tile([P, G, N], F32, name="y")
        hp_sb = sb.tile([P, G, N], F32, name="hp_sb")
        xh_sb = sb.tile([P, G, N], F32, name="xh_sb")
        rows_in = sb.tile([P, P], F32, name="rows_in", align_bytes=64)
        cols = sb.tile([P, P], F32, name="cols", align_bytes=64)
        half = sb.tile([P, P], F32, name="half", align_bytes=64)
        warm_in = sb.tile([P, 8], F32, name="warm_in")
        warm_out = sb.tile([P, 8], F32, name="warm_out")

        nc.gpsimd.memset(rows_in[:], 0.0)
        nc.gpsimd.memset(warm_in[:], 0.0)
        nc.scalar.activation(warm_out[:, 0:1], warm_in[:, 0:1], ACT.Tanh)

        wr_raw = load_operand("wr", wr)
        h_raw = [load_operand("h0", h[:, :, 0 : CHUNKS[0][1]])]
        for r, vec in enumerate((br, la, bi)):
            nc.sync.dma_start(
                out=rows_in[r:P:32, :].rearrange("q (g j) -> q g j", g=G),
                in_=vec.rearrange("g (q j) o -> q g (j o)", q=4),
            )
        h_raw.append(load_operand("h1", h[:, :, CHUNKS[1][0] : CHUNKS[1][1]]))
        wi_raw = load_operand("wi", wi)
        h_raw.append(load_operand("h2", h[:, :, CHUNKS[2][0] : CHUNKS[2][1]]))
        for g0 in (0, 2):
            nc.sync.dma_start(out=hp_sb[:, g0 : g0 + 2, :], in_=hp[g0 : g0 + 2].rearrange("g m n -> m g n"))
        for g0 in (0, 2):
            nc.sync.dma_start(out=xh_sb[:, g0 : g0 + 2, :], in_=xh[g0 : g0 + 2].rearrange("g m n -> m g n"))

        wr_mx = quantise("wr", interleave("wr", wr_raw))

        def param(r, g):
            return half[:, 32 * g + r : 32 * g + r + 1]

        def products(banks, w_mx, k):
            n0, n1 = CHUNKS[k]
            for c in range(0, n1 - n0, N_MM):
                for g in range(G):
                    gate_product(banks[g], g, w_mx, h_mx[k], n0, c)

        def decay(k):
            n0, n1 = CHUNKS[k]
            for g in range(G):
                nc.scalar.activation(t_r[:, g, n0:n1], z_r[g][:, n0:n1], ACT.Tanh, bias=param(0, g), scale=0.5)
            for g in range(G):
                nc.scalar.activation(a[:, g, n0:n1], t_r[:, g, n0:n1], ACT.Exp, bias=param(1, g), scale=param(1, g))

        def input_gate(n0, n1):
            for g in range(G):
                nc.scalar.activation(t_i[:, g, n0:n1], z_i[g][:, n0:n1], ACT.Tanh, bias=param(2, g), scale=0.5)

        split = CHUNKS[-1][0]
        h_mx = [quantise("h0", interleave("h0", h_raw[0]))]
        nc.scalar.activation(cols[:], rows_in[:], ACT.Copy, scale=0.5)
        nc.vector.transpose(half[:], cols[:])
        products(z_r, wr_mx, 0)
        decay(0)
        h_mx.append(quantise("h1", interleave("h1", h_raw[1])))
        products(z_r, wr_mx, 1)
        decay(1)
        wi_mx = quantise("wi", interleave("wi", wi_raw))
        products(z_i, wi_mx, 0)
        products(z_i, wi_mx, 1)
        input_gate(0, split)
        h_mx.append(quantise("h2", interleave("h2", h_raw[2])))
        products(z_r, wr_mx, 2)
        products(z_i, wi_mx, 2)
        decay(2)
        input_gate(split, N)

        def cap(g0, g1, n0, n1):
            nc.vector.tensor_scalar(a_cap[:, g0:g1, n0:n1], a[:, g0:g1, n0:n1], 1.0, None, ALU.min)

        def keep(g0, g1, n0, n1):
            nc.vector.tensor_tensor(kept[:, g0:g1, n0:n1], a[:, g0:g1, n0:n1], hp_sb[:, g0:g1, n0:n1], ALU.mult)

        def flat(t, c0, c1):
            return t[:].rearrange("p g n -> p (g n)")[:, c0:c1]

        def square(g0, g1, n0, n1):
            nc.vector.tensor_tensor(a_sq[:, g0:g1, n0:n1], a_cap[:, g0:g1, n0:n1], a_cap[:, g0:g1, n0:n1], ALU.mult)

        def gate(g0, g1, n0, n1):
            part = (slice(None), slice(g0, g1), slice(n0, n1))
            nc.vector.scalar_tensor_tensor(gated[part], t_i[part], 1.0, xh_sb[part], ALU.add, ALU.mult)

        cap(0, 4, 0, split)
        keep(0, 2, 0, split)
        square(0, 2, 0, split)
        keep(2, 4, 0, split)
        gate(0, 2, 0, split)
        cap(0, 2, split, N)
        keep(0, 2, split, N)
        square(0, 2, split, N)
        gate(2, 4, 0, split)
        cap(2, 4, split, N)
        keep(2, 4, split, N)
        gate(0, 4, split, N)

        edges = [sum(WIDTHS[:k]) for k in range(len(WIDTHS) + 1)]
        for step in SCALAR_TAIL:
            if step[0] == "q":
                nc.scalar.activation(flat(a_sq, step[1], step[2]), flat(a_cap, step[1], step[2]), ACT.Square)
            else:
                c0, c1 = edges[step[1]], edges[step[1] + 1]
                nc.scalar.activation(flat(root, c0, c1), flat(a_sq, c0, c1), ACT.Sqrt, bias=1.0, scale=-1.0)
        for kind, k in VECTOR_TAIL:
            c0, c1 = edges[k], edges[k + 1]
            if kind == "m":
                nc.vector.scalar_tensor_tensor(flat(fresh, c0, c1), flat(root, c0, c1), 0.5, flat(gated, c0, c1), ALU.mult, ALU.mult)
            else:
                nc.vector.tensor_tensor(flat(y, c0, c1), flat(fresh, c0, c1), flat(kept, c0, c1), ALU.add)
                for s0, s1 in STORES:
                    if c0 < s1 <= c1:
                        g = s0 // N
                        (nc.scalar if s1 == G * N else nc.sync).dma_start(out=out[g, :, s0 - g * N : s1 - g * N], in_=flat(y, s0, s1))
